import numpy as np
import ml_dtypes


def mxq(x, axis, fmt="e4m3"):
    dtype, down = {"e4m3": (ml_dtypes.float8_e4m3fn, 7), "e5m2": (ml_dtypes.float8_e5m2, 14)}[fmt]
    v = np.moveaxis(np.asarray(x, np.float32).astype(ml_dtypes.bfloat16).astype(np.float64), axis, -1)
    blocks = v.reshape(v.shape[:-1] + (-1, 32))
    amax = np.abs(blocks).max(-1, keepdims=True)
    byte = np.maximum(np.where(amax > 0, np.frexp(amax)[1] - 1 + 127, 0) - down, 1)
    scale = np.exp2(byte - 127.0)
    codes = (blocks / scale).astype(np.float32).astype(dtype).astype(np.float64)
    return np.moveaxis((codes * scale).reshape(v.shape), -1, axis)


WIDE = False


def mx_kscale(k):
    if not WIDE:
        return np.ones(k)
    levels = np.array([10, -10, 5, -5, 0])
    if k % 512:
        return np.exp2(np.random.permutation(np.resize(levels, k // 32))).repeat(32)
    a = np.empty((k // 512, 16))
    for p in range(k // 512):
        a[p, :8] = np.random.permutation(np.resize(levels, 8))
        for g in range(8):
            far = levels[np.abs(levels - a[p, g]) >= 10]
            a[p, g + 8] = far[np.random.randint(len(far))]
    return np.exp2(a.ravel()).repeat(32)


def f64(x):
    return np.asarray(x).astype(np.float64)


def striped(idx):
    return np.tile(np.asarray(idx).reshape(-1, 16).T, (8, 1)).astype(np.uint16)


def unstriped(offs):
    return offs[:16].T.reshape(-1).astype(np.int64)


E2M1 = np.array([0.0, 0.5, 1.0, 1.5, 2.0, 3.0, 4.0, 6.0, -0.0, -0.5, -1.0, -1.5, -2.0, -3.0, -4.0, -6.0])


def pack_weight(w, fmt):
    k, n = w.shape
    w = f64(np.asarray(w, np.float32).astype(ml_dtypes.bfloat16)).reshape(k // 32, 32, n)
    amax = np.abs(w).max(1)
    if fmt == "e4m3":
        byte = np.frexp(amax)[1] - 1 + 127 - 7
    else:
        mant, ex = np.frexp(amax / 6.0)
        byte = np.where(mant > 0.5, ex, ex - 1) + 127
    byte = np.clip(np.where(amax > 0, byte, 1), 1, 254)
    scaled = (w * np.exp2(127.0 - byte)[:, None, :]).reshape(k, n).astype(np.float32)
    by_word = np.ascontiguousarray(scaled.reshape(k // 512, 128, 4, n).transpose(0, 1, 3, 2))
    if fmt == "e4m3":
        words = by_word.astype(ml_dtypes.float8_e4m3fn).view(np.uint8)
    else:
        c = by_word.astype(ml_dtypes.float4_e2m1fn).view(np.uint8) & 0xF
        words = (c[..., 0::2] | (c[..., 1::2] << 4)).reshape(k // 512, 128, 2 * n)
    return np.ascontiguousarray(words), np.ascontiguousarray(byte.astype(np.uint8).reshape(k // 512, 16, n))


def unpack_weight(words, scales, fmt):
    g, _, n = scales.shape
    words = np.ascontiguousarray(words).reshape(g, 128, n, -1)
    if fmt == "e4m3":
        vals = words.view(ml_dtypes.float8_e4m3fn).astype(np.float64)
    else:
        nib = np.empty((g, 128, n, 4), np.uint8)
        nib[..., 0::2] = words & 0xF
        nib[..., 1::2] = words >> 4
        vals = E2M1[nib]
    vals = vals * np.repeat(np.exp2(scales.astype(np.float64) - 127.0), 8, axis=1)[..., None]
    return vals.transpose(0, 1, 3, 2).reshape(g * 512, n)


def softplus(v):
    return np.log(1.0 + np.exp(v))


D, E, T, I, Q = 512, 512, 1024, 256, 512


def setup_inputs():
    n = np.random.standard_normal
    idx = np.random.permutation(T)[:I]
    fd = mx_kscale(D)
    fq = mx_kscale(Q)
    keysp = pack_weight(n((D, T)) / fd[:, None], "e2m1")
    return {
        "query": (n((D, Q)) * 1.0 / np.sqrt(D) * fd[:, None]).astype(np.float32),
        "keys_words": keysp[0],
        "keys_scales": keysp[1],
        "th": (np.random.uniform(-0.5, 0.5, (Q, 1))).astype(np.float32),
        "reserve": (np.random.uniform(20.0, 100.0, (Q, 1))).astype(np.float32),
        "size": (np.random.uniform(0.5, 2.0, (1, I))).astype(np.float32),
        "qs": (np.random.uniform(2.0, 8.0, (Q, 1)) * fq[:, None]).astype(np.float32),
        "grows": (n((Q, E)) / fq[:, None]).astype(np.float32),
        "old": (n((E, T)) * 2.0).astype(np.float32),
        "fade": (np.random.uniform(0.5, 1.0, (1, T))).astype(np.float32),
        "offs": striped(idx),
    }


def reference(query, keys_words, keys_scales, th, reserve, size, qs, grows, old, fade, offs):
    idx = unstriped(offs)
    keysu = unpack_weight(keys_words, keys_scales, "e2m1")
    queryq = mxq(f64(query), 0, "e4m3")
    keysidxg = keysu[:, idx]
    a = queryq.T @ keysidxg
    p = softplus(a - f64(th))
    z = np.sum(p, axis=1, keepdims=True) + f64(reserve)
    w = p * f64(size) / z
    wq = w * f64(qs)
    growsq = mxq(f64(grows), 0, "e4m3")
    wqq = mxq(wq, 0, "e4m3")
    gv = growsq.T @ wqq
    gf = np.zeros((E, T))
    gf[:, idx] = gv
    y = f64(old) * f64(fade) + gf
    return y

@@ -1,0 +1,239 @@
+from contextlib import ExitStack
+
+import concourse.mybir as mybir
+from concourse.masks import make_identity
+
+D, E, T, I, Q = 512, 512, 1024, 256, 512
+FLOPS = 2 * D * Q * I + 2 * Q * E * I
+
+F32 = mybir.dt.float32
+BF16 = mybir.dt.bfloat16
+I32 = mybir.dt.int32
+U32 = mybir.dt.uint32
+U16 = mybir.dt.uint16
+U8 = mybir.dt.uint8
+FP8X4 = mybir.dt.float8_e4m3fn_x4
+FP4X4 = mybir.dt.float4_e2m1fn_x4
+ALU = mybir.AluOpType
+ACT = mybir.ActivationFunctionType
+
+P = 128
+PACK = 4
+BANK = 512
+CHUNKS = T // P
+TINY = 2.0**-60
+
+
+def tile_attend_bsoftthreshold_v_kernel(tc, query, keys_words, keys_scales, th, reserve, size, qs, grows, old, fade, offs, out):
+    nc = tc.nc
+    with ExitStack() as ctx:
+        keep = ctx.enter_context(tc.tile_pool(name="keep", bufs=1))
+        psum = ctx.enter_context(tc.psum_pool(name="psum", bufs=1))
+
+        offsets = keep.tile([P, I // 16], U16, name="offsets")
+        key_words = keep.tile([P, T], U16, name="key_words")
+        key_scales = keep.tile([P, T], U8, name="key_scales")
+        rows = keep.tile([P, P], F32, name="rows")
+        ident = keep.tile([P, P], F32, name="ident")
+        windows = [keep.tile([P, T], F32, name="window%d" % k) for k in range(3)]
+        q_raw = [keep.tile([P, PACK, Q // 2], F32, name="q_raw%d" % h) for h in range(2)]
+        g_raw = [keep.tile([P, PACK, E // 2], F32, name="g_raw%d" % h) for h in range(2)]
+        old_sb = [keep.tile([P, T], F32, name="old%d" % j) for j in range(4)]
+        th_sb = keep.tile([P, PACK], F32, name="th_sb")
+        res_sb = keep.tile([P, PACK], F32, name="res_sb")
+        qs_sb = keep.tile([P, PACK], F32, name="qs_sb")
+
+        nc.vector.memset(key_scales[:].bitcast(I32), 0)
+        nc.vector.memset(rows[:], 0.0)
+        make_identity(nc, ident[:])
+
+        q_view = query.rearrange("(p j) q -> p j q", j=PACK)
+        g_view = grows.rearrange("(p j) e -> p j e", j=PACK)
+        nc.sync.dma_start(q_raw[0][:], q_view[:, :, 0 : Q // 2])
+        nc.sync.dma_start(key_words[:].bitcast(I32), keys_words[0].bitcast(I32))
+        nc.sync.dma_start(offsets[:], offs)
+        nc.sync.dma_start(q_raw[1][:], q_view[:, :, Q // 2 : Q])
+        for quad in range(4):
+            nc.scalar.dma_start(
+                key_scales[32 * quad : 32 * quad + 4, :].bitcast(I32),
+                keys_scales[0, 4 * quad : 4 * quad + 4, :].bitcast(I32),
+            )
+        nc.gpsimd.dma_start(th_sb[:], th.rearrange("(s r) o -> s (r o)", r=PACK))
+        nc.gpsimd.dma_start(rows[0:CHUNKS, :], fade.rearrange("o (c p) -> (o c) p", p=P))
+        nc.gpsimd.dma_start(rows[CHUNKS : CHUNKS + 2, :], size.rearrange("o (c p) -> (o c) p", p=P))
+        nc.gpsimd.dma_start(qs_sb[:], qs.rearrange("(s r) o -> s (r o)", r=PACK))
+        nc.gpsimd.dma_start(res_sb[:], reserve.rearrange("(s r) o -> s (r o)", r=PACK))
+        for h in range(2):
+            nc.sync.dma_start(g_raw[h][:], g_view[:, :, h * (E // 2) : (h + 1) * (E // 2)])
+        for j in range(4):
+            nc.sync.dma_start(old_sb[j][:], old[j * P : (j + 1) * P, :])
+
+        for k in range(3):
+            nc.vector.memset(windows[k][:], 0.0)
+
+        warm = keep.tile([P, PACK], F32, name="warm")
+        nc.scalar.activation(warm[:], ident[:, 0:PACK], ACT.Sigmoid)
+
+        key_words_g = keep.tile([P, I], U16, name="key_words_g", align_bytes=64)
+        key_scales_g = keep.tile([P, I], U8, name="key_scales_g", align_bytes=64)
+        nc.vector.tensor_copy(key_words_g[:], key_words[:].indirect(offsets[:]))
+
+        turned = psum.tile([P, P], F32, name="turned", tag="m")
+        nc.tensor.transpose(turned[:], rows[:], ident[:])
+        cols = keep.tile([P, 16], F32, name="cols")
+        nc.vector.tensor_copy(cols[:], turned[:, 0:16])
+        size_b = psum.tile([P, I], F32, name="size_b", tag="n")
+        for c in range(2):
+            nc.tensor.transpose(size_b[:, c * P : (c + 1) * P], cols[:, CHUNKS + c : CHUNKS + c + 1].to_broadcast([P, P]), ident[:])
+        fade_b = [psum.tile([P, BANK], F32, name="fade_b%d" % h, tag="f%d" % h) for h in range(2)]
+        for c in range(CHUNKS):
+            nc.tensor.transpose(fade_b[c // 4][:, (c % 4) * P : (c % 4 + 1) * P], cols[:, c : c + 1].to_broadcast([P, P]), ident[:])
+        size_qs = keep.tile([P, PACK, I], F32, name="size_qs")
+        for r in range(PACK):
+            nc.scalar.activation(size_qs[:, r, :], size_b[:], ACT.Copy, scale=qs_sb[:, r : r + 1])
+
+        q_grouped = keep.tile([P, PACK, P, PACK], BF16, name="q_grouped", align_bytes=64)
+        q_codes = keep.tile([P, Q], U32, name="q_codes", align_bytes=64)
+        q_scales = keep.tile([P, Q], U8, name="q_scales", align_bytes=64)
+
+        def deal_query(h, pair):
+            nc.vector.tensor_scalar(
+                q_grouped[:, 2 * pair : 2 * pair + 2, 64 * h : 64 * h + 64, :].rearrange("p r s j -> p s j r"),
+                q_raw[h][:].rearrange("p j (s r) -> p s j r", r=PACK)[:, :, :, 2 * pair : 2 * pair + 2],
+                -1.0,
+                None,
+                ALU.mult,
+            )
+
+        deal_query(0, 0)
+        deal_query(0, 1)
+        nc.vector.tensor_copy(key_scales_g[:], key_scales[:].indirect(offsets[:]))
+        deal_query(1, 0)
+        deal_query(1, 1)
+        for pair in range(2):
+            nc.vector.quantize_mx(
+                out=q_codes[:, 256 * pair : 256 * (pair + 1)].bitcast(FP8X4),
+                scales=q_scales[:, 256 * pair : 256 * (pair + 1)],
+                in_=q_grouped[:, 2 * pair : 2 * pair + 2, :, :].rearrange("p r s j -> p (r s j)"),
+            )
+
+        score_tags = ["s0", "s1", "ta", "tb"]
+        scores = [psum.tile([P, I], F32, name="scores%d" % r, tag=score_tags[r]) for r in range(PACK)]
+        sig = keep.tile([P, PACK, I], F32, name="sig")
+        for r in range(PACK):
+            nc.tensor.matmul_mx(
+                out=scores[r][:],
+                lhsT=q_codes[:, r * P : (r + 1) * P].bitcast(FP8X4),
+                lhsT_scale=q_scales[:, r * P : (r + 1) * P],
+                rhs=key_words_g[:].bitcast(FP4X4),
+                rhs_scale=key_scales_g[:],
+                start=True,
+                stop=True,
+            )
+            nc.scalar.activation(sig[:, r, :], scores[r][:], ACT.Sigmoid, bias=th_sb[:, r : r + 1])
+
+        g_grouped = keep.tile([P, E, PACK], BF16, name="g_grouped", align_bytes=64)
+        g_codes = keep.tile([P, E], U32, name="g_codes", align_bytes=64)
+        g_scales = keep.tile([P, E], U8, name="g_scales", align_bytes=64)
+        for h in range(2):
+            nc.vector.tensor_copy(
+                g_grouped[:, 256 * h : 256 * (h + 1), :].rearrange("p (c i) j -> p c j i", i=4),
+                g_raw[h][:].rearrange("p j (c i) -> p c j i", i=4),
+            )
+        nc.vector.quantize_mx(out=g_codes[:].bitcast(FP8X4), scales=g_scales[:], in_=g_grouped[:].rearrange("p e j -> p (e j)"))
+        for h in range(2):
+            half = slice(h * BANK, (h + 1) * BANK)
+            nc.vector.tensor_tensor(old_sb[0][:, half], old_sb[0][:, half], fade_b[h][:], ALU.mult)
+
+        logs = keep.tile([P, PACK, I], F32, name="logs")
+        neg_p = keep.tile([P, PACK, I], F32, name="neg_p")
+        neg_sum = keep.tile([P, PACK], F32, name="neg_sum")
+        neg_z = keep.tile([P, PACK], F32, name="neg_z")
+        neg_rz = keep.tile([P, PACK], F32, name="neg_rz")
+        w_planes = keep.tile([P, PACK, I], BF16, name="w_planes")
+        for r in range(PACK):
+            nc.scalar.activation(logs[:, r, :], sig[:, r, :], ACT.Ln, bias=TINY)
+
+        def parts(r):
+            nc.vector.scalar_tensor_tensor(
+                neg_p[:, r, :], scores[r][:], th_sb[:, r : r + 1], logs[:, r, :], ALU.add, ALU.min, accum_out=neg_sum[:, r : r + 1]
+            )
+
+        def add_reserve(pair):
+            two = slice(2 * pair, 2 * pair + 2)
+            nc.vector.tensor_tensor(neg_z[:, two], neg_sum[:, two], res_sb[:, two], ALU.subtract)
+
+        def invert(pair):
+            two = slice(2 * pair, 2 * pair + 2)
+            nc.vector.reciprocal(neg_rz[:, two], neg_z[:, two])
+
+        def weights(r):
+            nc.vector.scalar_tensor_tensor(w_planes[:, r, :], neg_p[:, r, :], neg_rz[:, r : r + 1], size_qs[:, r, :], ALU.mult, ALU.mult)
+
+        parts(0)
+        parts(1)
+        parts(2)
+        add_reserve(0)
+        parts(3)
+        invert(0)
+        add_reserve(1)
+        weights(0)
+        invert(1)
+        weights(1)
+        weights(2)
+        weights(3)
+        w_grouped = keep.tile([P, I, PACK], BF16, name="w_grouped", align_bytes=64)
+        w_codes = keep.tile([P, I], U32, name="w_codes", align_bytes=64)
+        w_scales = keep.tile([P, I], U8, name="w_scales", align_bytes=64)
+        nc.vector.tensor_copy(
+            w_grouped[:].rearrange("p (c i) r -> p c r i", i=4),
+            w_planes[:].rearrange("p r (c i) -> p c r i", i=4),
+        )
+        nc.vector.quantize_mx(out=w_codes[:].bitcast(FP8X4), scales=w_scales[:], in_=w_grouped[:].rearrange("p i r -> p (i r)"))
+
+        faded_t = keep.tile([P, CHUNKS, 3, P], F32, name="faded_t")
+        turn_tags = ["m", "n", "ta", "tb"]
+        for c in range(CHUNKS):
+            bank = psum.tile([P, 3, P], F32, name="old_t%d" % c, tag=turn_tags[c % 4])
+            for j in range(1, 4):
+                nc.tensor.transpose(bank[:, j - 1, :], old_sb[j][:, c * P : (c + 1) * P], ident[:])
+            nc.scalar.activation(faded_t[:, c, :, :], bank[:], ACT.Copy, scale=cols[:, c : c + 1])
+
+        gv_sb = [keep.tile([P, I], F32, name="gv%d" % j) for j in range(4)]
+        for j in range(4):
+            gv = psum.tile([P, I], F32, name="gv_ps%d" % j, tag="s%d" % (j % 2))
+            nc.tensor.matmul_mx(
+                out=gv[:],
+                lhsT=g_codes[:, j * P : (j + 1) * P].bitcast(FP8X4),
+                lhsT_scale=g_scales[:, j * P : (j + 1) * P],
+                rhs=w_codes[:].bitcast(FP8X4),
+                rhs_scale=w_scales[:],
+                start=True,
+                stop=True,
+            )
+            nc.scalar.copy(gv_sb[j][:], gv[:])
+
+        back_tags = {1: ["ta", "tb"], 2: ["f0", "f1"], 3: ["m", "n"]}
+        faded = {}
+        for j in range(1, 4):
+            for h in range(2):
+                bank = psum.tile([P, BANK], F32, name="faded%d_%d" % (j, h), tag=back_tags[j][h])
+                for c in range(4):
+                    nc.tensor.transpose(bank[:, c * P : (c + 1) * P], faded_t[:, 4 * h + c, j - 1, :], ident[:])
+                faded[j, h] = bank
+        result = [keep.tile([P, T], F32, name="result%d" % j) for j in range(1, 4)]
+        for h in range(2):
+            nc.scalar.copy(result[0][:, h * BANK : (h + 1) * BANK], faded[1, h][:])
+
+        for j in range(4):
+            window = windows[j % 3]
+            nc.vector.tensor_copy(window[:].indirect(offsets[:]), gv_sb[j][:])
+            for h in range(2):
+                half = slice(h * BANK, (h + 1) * BANK)
+                if j < 2:
+                    dst = old_sb[0] if j == 0 else result[0]
+                    nc.gpsimd.tensor_tensor(dst[:, half], dst[:, half], window[:, half], ALU.add)
+                else:
+                    dst = result[j - 1]
+                    nc.vector.tensor_tensor(dst[:, half], faded[j, h][:], window[:, half], ALU.add)
+                nc.sync.dma_start(out[j * P : (j + 1) * P, half], dst[:, half])

@@ -1,7 +1,6 @@
 from contextlib import ExitStack
 
 import concourse.mybir as mybir
-from concourse.masks import make_identity
 
 D, E, T, I, Q = 512, 512, 1024, 256, 512
 FLOPS = 2 * D * Q * I + 2 * Q * E * I
@@ -31,48 +30,45 @@ def tile_attend_bsoftthreshold_v_kernel(tc, query, keys_words, keys_scales, th, 
         psum = ctx.enter_context(tc.psum_pool(name="psum", bufs=1))
 
         offsets = keep.tile([P, I // 16], U16, name="offsets")
-        key_words = keep.tile([P, T], U16, name="key_words")
-        key_scales = keep.tile([P, T], U8, name="key_scales")
-        rows = keep.tile([P, P], F32, name="rows")
+        key_words = keep.tile([P, T], U16, name="key_words", tag="early_a")
+        key_scales = keep.tile([P, T], U8, name="key_scales", tag="early_s")
+        rows = keep.tile([P, P], F32, name="rows", tag="early_g")
         ident = keep.tile([P, P], F32, name="ident")
-        windows = [keep.tile([P, T], F32, name="window%d" % k) for k in range(3)]
-        q_raw = [keep.tile([P, PACK, Q // 2], F32, name="q_raw%d" % h) for h in range(2)]
-        g_raw = [keep.tile([P, PACK, E // 2], F32, name="g_raw%d" % h) for h in range(2)]
-        old_sb = [keep.tile([P, T], F32, name="old%d" % j) for j in range(4)]
+        q_raw = [keep.tile([P, PACK, Q // 2], F32, name="q_raw%d" % h, tag="early_q%d" % h) for h in range(2)]
         th_sb = keep.tile([P, PACK], F32, name="th_sb")
-        res_sb = keep.tile([P, PACK], F32, name="res_sb")
-        qs_sb = keep.tile([P, PACK], F32, name="qs_sb")
 
         nc.vector.memset(key_scales[:].bitcast(I32), 0)
-        nc.vector.memset(rows[:], 0.0)
-        make_identity(nc, ident[:])
+        warm_in = keep.tile([P, 1], F32, name="warm_in")
+        nc.vector.memset(warm_in[:], 0.0)
+        ones = keep.tile([P, P], F32, name="ones")
+        count = keep.tile([P, P], F32, name="count", align_bytes=64, tag="count_window")
+        count_t = keep.tile([P, 32], F32, name="count_t", align_bytes=64)
+        nc.vector.memset(ones[:], 1.0)
+        nc.vector.tensor_tensor_scan(count[:], ones[:], ones[:], 0.0, ALU.mult, ALU.add)
+        nc.vector.transpose(count_t[:], count[:, 0:32])
+        for quad in range(4):
+            part = slice(32 * quad, 32 * quad + 32)
+            nc.vector.tensor_scalar(ident[part, :], count[part, :], -32.0 * quad, count_t[part, 0:1], ALU.add, ALU.is_equal)
+        windows = [keep.tile([P, T], F32, name="window0", align_bytes=64, tag="count_window")]
+        nc.vector.memset(windows[0][:], 0.0)
 
         q_view = query.rearrange("(p j) q -> p j q", j=PACK)
         g_view = grows.rearrange("(p j) e -> p j e", j=PACK)
-        nc.sync.dma_start(q_raw[0][:], q_view[:, :, 0 : Q // 2])
-        nc.sync.dma_start(key_words[:].bitcast(I32), keys_words[0].bitcast(I32))
         nc.sync.dma_start(offsets[:], offs)
+        nc.sync.dma_start(key_words[:].bitcast(I32), keys_words[0].bitcast(I32))
+        nc.sync.dma_start(q_raw[0][:], q_view[:, :, 0 : Q // 2])
         nc.sync.dma_start(q_raw[1][:], q_view[:, :, Q // 2 : Q])
+        nc.scalar.dma_start(rows[0:CHUNKS, :], fade.rearrange("o (c p) -> (o c) p", p=P))
+        nc.scalar.dma_start(rows[CHUNKS : CHUNKS + 2, :], size.rearrange("o (c p) -> (o c) p", p=P))
         for quad in range(4):
             nc.scalar.dma_start(
                 key_scales[32 * quad : 32 * quad + 4, :].bitcast(I32),
                 keys_scales[0, 4 * quad : 4 * quad + 4, :].bitcast(I32),
             )
-        nc.gpsimd.dma_start(th_sb[:], th.rearrange("(s r) o -> s (r o)", r=PACK))
-        nc.gpsimd.dma_start(rows[0:CHUNKS, :], fade.rearrange("o (c p) -> (o c) p", p=P))
-        nc.gpsimd.dma_start(rows[CHUNKS : CHUNKS + 2, :], size.rearrange("o (c p) -> (o c) p", p=P))
-        nc.gpsimd.dma_start(qs_sb[:], qs.rearrange("(s r) o -> s (r o)", r=PACK))
-        nc.gpsimd.dma_start(res_sb[:], reserve.rearrange("(s r) o -> s (r o)", r=PACK))
-        for h in range(2):
-            nc.sync.dma_start(g_raw[h][:], g_view[:, :, h * (E // 2) : (h + 1) * (E // 2)])
-        for j in range(4):
-            nc.sync.dma_start(old_sb[j][:], old[j * P : (j + 1) * P, :])
+        nc.scalar.dma_start(th_sb[:], th.rearrange("(s r) o -> s (r o)", r=PACK))
+        warm = keep.tile([P, 1], F32, name="warm")
+        nc.scalar.activation(warm[:], warm_in[:], ACT.Sigmoid)
 
-        for k in range(3):
-            nc.vector.memset(windows[k][:], 0.0)
-
-        warm = keep.tile([P, PACK], F32, name="warm")
-        nc.scalar.activation(warm[:], ident[:, 0:PACK], ACT.Sigmoid)
 
         key_words_g = keep.tile([P, I], U16, name="key_words_g", align_bytes=64)
         key_scales_g = keep.tile([P, I], U8, name="key_scales_g", align_bytes=64)
@@ -80,36 +76,43 @@ def tile_attend_bsoftthreshold_v_kernel(tc, query, keys_words, keys_scales, th, 
 
         turned = psum.tile([P, P], F32, name="turned", tag="m")
         nc.tensor.transpose(turned[:], rows[:], ident[:])
-        cols = keep.tile([P, 16], F32, name="cols")
-        nc.vector.tensor_copy(cols[:], turned[:, 0:16])
+        g_raw = [keep.tile([P, PACK, E // 2], F32, name="g_raw%d" % h, tag=["early_g", "early_a"][h]) for h in range(2)]
+        for h in range(2):
+            nc.sync.dma_start(g_raw[h][:], g_view[:, :, h * (E // 2) : (h + 1) * (E // 2)])
+        cols = keep.tile([P, CHUNKS + 2], F32, name="cols")
+        nc.vector.tensor_copy(cols[:], turned[:, 0 : CHUNKS + 2])
         size_b = psum.tile([P, I], F32, name="size_b", tag="n")
         for c in range(2):
             nc.tensor.transpose(size_b[:, c * P : (c + 1) * P], cols[:, CHUNKS + c : CHUNKS + c + 1].to_broadcast([P, P]), ident[:])
         fade_b = [psum.tile([P, BANK], F32, name="fade_b%d" % h, tag="f%d" % h) for h in range(2)]
         for c in range(CHUNKS):
             nc.tensor.transpose(fade_b[c // 4][:, (c % 4) * P : (c % 4 + 1) * P], cols[:, c : c + 1].to_broadcast([P, P]), ident[:])
-        size_qs = keep.tile([P, PACK, I], F32, name="size_qs")
-        for r in range(PACK):
-            nc.scalar.activation(size_qs[:, r, :], size_b[:], ACT.Copy, scale=qs_sb[:, r : r + 1])
 
         q_grouped = keep.tile([P, PACK, P, PACK], BF16, name="q_grouped", align_bytes=64)
-        q_codes = keep.tile([P, Q], U32, name="q_codes", align_bytes=64)
+        q_codes = keep.tile([P, Q], U32, name="q_codes", align_bytes=64, tag="codes_logs")
         q_scales = keep.tile([P, Q], U8, name="q_scales", align_bytes=64)
 
         def deal_query(h, pair):
-            nc.vector.tensor_scalar(
-                q_grouped[:, 2 * pair : 2 * pair + 2, 64 * h : 64 * h + 64, :].rearrange("p r s j -> p s j r"),
-                q_raw[h][:].rearrange("p j (s r) -> p s j r", r=PACK)[:, :, :, 2 * pair : 2 * pair + 2],
-                -1.0,
-                None,
-                ALU.mult,
-            )
+            dst = q_grouped[:, 2 * pair : 2 * pair + 2, 64 * h : 64 * h + 64, :].rearrange("p r s j -> p s j r")
+            src = q_raw[h][:].rearrange("p j (s r) -> p s j r", r=PACK)[:, :, :, 2 * pair : 2 * pair + 2]
+            if pair == 0 or h == 0:
+                nc.vector.tensor_scalar(dst, src, -1.0, None, ALU.mult)
+            else:
+                nc.scalar.activation(dst, src, ACT.Copy, scale=-1.0)
 
         deal_query(0, 0)
         deal_query(0, 1)
         nc.vector.tensor_copy(key_scales_g[:], key_scales[:].indirect(offsets[:]))
         deal_query(1, 0)
         deal_query(1, 1)
+        old_sb = [keep.tile([P, T], F32, name="old%d" % j, tag="early_q%d" % j) for j in range(2)]
+        for j in range(2):
+            nc.sync.dma_start(old_sb[j][:], old[j * P : (j + 1) * P, :])
+        vectors = keep.tile([P, 2, 8], F32, name="vectors", tag="early_s")
+        res_sb = vectors[:, 0, 0:PACK]
+        qs_sb = vectors[:, 1, 0:PACK]
+        nc.sync.dma_start(res_sb, reserve.rearrange("(s r) o -> s (r o)", r=PACK))
+        nc.sync.dma_start(qs_sb, qs.rearrange("(s r) o -> s (r o)", r=PACK))
         for pair in range(2):
             nc.vector.quantize_mx(
                 out=q_codes[:, 256 * pair : 256 * (pair + 1)].bitcast(FP8X4),
@@ -119,7 +122,7 @@ def tile_attend_bsoftthreshold_v_kernel(tc, query, keys_words, keys_scales, th, 
 
         score_tags = ["s0", "s1", "ta", "tb"]
         scores = [psum.tile([P, I], F32, name="scores%d" % r, tag=score_tags[r]) for r in range(PACK)]
-        sig = keep.tile([P, PACK, I], F32, name="sig")
+        sig = keep.tile([P, PACK, I], F32, name="sig", tag="sig_fade")
         for r in range(PACK):
             nc.tensor.matmul_mx(
                 out=scores[r][:],
@@ -132,7 +135,7 @@ def tile_attend_bsoftthreshold_v_kernel(tc, query, keys_words, keys_scales, th, 
             )
             nc.scalar.activation(sig[:, r, :], scores[r][:], ACT.Sigmoid, bias=th_sb[:, r : r + 1])
 
-        g_grouped = keep.tile([P, E, PACK], BF16, name="g_grouped", align_bytes=64)
+        g_grouped = keep.tile([P, E, PACK], BF16, name="g_grouped", align_bytes=64, tag="grouped_window")
         g_codes = keep.tile([P, E], U32, name="g_codes", align_bytes=64)
         g_scales = keep.tile([P, E], U8, name="g_scales", align_bytes=64)
         for h in range(2):
@@ -140,19 +143,27 @@ def tile_attend_bsoftthreshold_v_kernel(tc, query, keys_words, keys_scales, th, 
                 g_grouped[:, 256 * h : 256 * (h + 1), :].rearrange("p (c i) j -> p c j i", i=4),
                 g_raw[h][:].rearrange("p j (c i) -> p c j i", i=4),
             )
+        old_late = keep.tile([P, 2, T], F32, name="old_late", tag="early_g")
+        nc.sync.dma_start(old_late[:], old[2 * P : 4 * P, :].rearrange("(j p) t -> p j t", p=P))
         nc.vector.quantize_mx(out=g_codes[:].bitcast(FP8X4), scales=g_scales[:], in_=g_grouped[:].rearrange("p e j -> p (e j)"))
+        windows.append(keep.tile([P, T], F32, name="window1", align_bytes=64, tag="grouped_window"))
+        nc.gpsimd.memset(windows[1][:], 0.0)
         for h in range(2):
             half = slice(h * BANK, (h + 1) * BANK)
             nc.vector.tensor_tensor(old_sb[0][:, half], old_sb[0][:, half], fade_b[h][:], ALU.mult)
 
-        logs = keep.tile([P, PACK, I], F32, name="logs")
+        logs = keep.tile([P, PACK, I], F32, name="logs", align_bytes=64, tag="codes_logs")
         neg_p = keep.tile([P, PACK, I], F32, name="neg_p")
         neg_sum = keep.tile([P, PACK], F32, name="neg_sum")
         neg_z = keep.tile([P, PACK], F32, name="neg_z")
         neg_rz = keep.tile([P, PACK], F32, name="neg_rz")
+        neg_c = keep.tile([P, PACK], F32, name="neg_c")
         w_planes = keep.tile([P, PACK, I], BF16, name="w_planes")
         for r in range(PACK):
             nc.scalar.activation(logs[:, r, :], sig[:, r, :], ACT.Ln, bias=TINY)
+        fade_sb = keep.tile([P, T], F32, name="fade_sb", tag="sig_fade")
+        for h in range(2):
+            nc.scalar.copy(fade_sb[:, h * BANK : (h + 1) * BANK], fade_b[h][:])
 
         def parts(r):
             nc.vector.scalar_tensor_tensor(
@@ -167,73 +178,130 @@ def tile_attend_bsoftthreshold_v_kernel(tc, query, keys_words, keys_scales, th, 
             two = slice(2 * pair, 2 * pair + 2)
             nc.vector.reciprocal(neg_rz[:, two], neg_z[:, two])
 
-        def weights(r):
-            nc.vector.scalar_tensor_tensor(w_planes[:, r, :], neg_p[:, r, :], neg_rz[:, r : r + 1], size_qs[:, r, :], ALU.mult, ALU.mult)
+        def row_scale(pair):
+            two = slice(2 * pair, 2 * pair + 2)
+            nc.vector.tensor_tensor(neg_c[:, two], neg_rz[:, two], qs_sb[:, two], ALU.mult)
+
+        def weights(r, h):
+            slots = slice(h * P, (h + 1) * P)
+            nc.vector.scalar_tensor_tensor(w_planes[:, r, slots], neg_p[:, r, slots], neg_c[:, r : r + 1], size_b[:, slots], ALU.mult, ALU.mult)
+
+        w_grouped = keep.tile([P, I, PACK], BF16, name="w_grouped", align_bytes=64, tag="w_then_x1")
+        w_codes = keep.tile([P, I], U32, name="w_codes", align_bytes=64)
+        w_scales = keep.tile([P, I], U8, name="w_scales", align_bytes=64)
+
+        def interleave(h):
+            slots = slice(h * P, (h + 1) * P)
+            nc.vector.tensor_copy(
+                w_grouped[:, slots, :].rearrange("p (c i) r -> p c r i", i=4),
+                w_planes[:, :, slots].rearrange("p r (c i) -> p c r i", i=4),
+            )
+
+        def quantise(h):
+            slots = slice(h * P, (h + 1) * P)
+            nc.vector.quantize_mx(
+                out=w_codes[:, slots].bitcast(FP8X4), scales=w_scales[:, slots], in_=w_grouped[:, slots, :].rearrange("p i r -> p (i r)")
+            )
 
         parts(0)
         parts(1)
-        parts(2)
         add_reserve(0)
-        parts(3)
+        parts(2)
         invert(0)
+        parts(3)
+        windows.append(keep.tile([P, T], F32, name="window2", align_bytes=64, tag="codes_logs"))
+        nc.gpsimd.memset(windows[2][:], 0.0)
+        row_scale(0)
         add_reserve(1)
-        weights(0)
+        weights(0, 0)
         invert(1)
-        weights(1)
-        weights(2)
-        weights(3)
-        w_grouped = keep.tile([P, I, PACK], BF16, name="w_grouped", align_bytes=64)
-        w_codes = keep.tile([P, I], U32, name="w_codes", align_bytes=64)
-        w_scales = keep.tile([P, I], U8, name="w_scales", align_bytes=64)
-        nc.vector.tensor_copy(
-            w_grouped[:].rearrange("p (c i) r -> p c r i", i=4),
-            w_planes[:].rearrange("p r (c i) -> p c r i", i=4),
-        )
-        nc.vector.quantize_mx(out=w_codes[:].bitcast(FP8X4), scales=w_scales[:], in_=w_grouped[:].rearrange("p i r -> p (i r)"))
-
-        faded_t = keep.tile([P, CHUNKS, 3, P], F32, name="faded_t")
-        turn_tags = ["m", "n", "ta", "tb"]
-        for c in range(CHUNKS):
-            bank = psum.tile([P, 3, P], F32, name="old_t%d" % c, tag=turn_tags[c % 4])
-            for j in range(1, 4):
-                nc.tensor.transpose(bank[:, j - 1, :], old_sb[j][:, c * P : (c + 1) * P], ident[:])
-            nc.scalar.activation(faded_t[:, c, :, :], bank[:], ACT.Copy, scale=cols[:, c : c + 1])
+        weights(1, 0)
+        row_scale(1)
+        weights(0, 1)
+        weights(2, 0)
+        weights(3, 0)
+        weights(1, 1)
+        interleave(0)
+        weights(2, 1)
+        weights(3, 1)
+        quantise(0)
+        interleave(1)
+        quantise(1)
 
         gv_sb = [keep.tile([P, I], F32, name="gv%d" % j) for j in range(4)]
-        for j in range(4):
-            gv = psum.tile([P, I], F32, name="gv_ps%d" % j, tag="s%d" % (j % 2))
+        gv_tags = ["s0", "s1", "ta", "tb"]
+
+        def gradient(j, slots, tag):
+            gv = psum.tile([P, slots.stop - slots.start], F32, name="gv_ps%d_%d" % (j, slots.start), tag=tag)
             nc.tensor.matmul_mx(
                 out=gv[:],
                 lhsT=g_codes[:, j * P : (j + 1) * P].bitcast(FP8X4),
                 lhsT_scale=g_scales[:, j * P : (j + 1) * P],
-                rhs=w_codes[:].bitcast(FP8X4),
-                rhs_scale=w_scales[:],
+                rhs=w_codes[:, slots].bitcast(FP8X4),
+                rhs_scale=w_scales[:, slots],
                 start=True,
                 stop=True,
             )
-            nc.scalar.copy(gv_sb[j][:], gv[:])
+            nc.scalar.copy(gv_sb[j][:, slots], gv[:])
 
-        back_tags = {1: ["ta", "tb"], 2: ["f0", "f1"], 3: ["m", "n"]}
-        faded = {}
+        gradient(0, slice(0, P), "s0")
+        gradient(0, slice(P, I), "n")
         for j in range(1, 4):
+            gradient(j, slice(0, I), gv_tags[j])
+
+        faded1 = keep.tile([P, T], F32, name="faded1", align_bytes=64, tag="w_then_x1")
+        for h in range(2):
+            half = slice(h * BANK, (h + 1) * BANK)
+            nc.gpsimd.tensor_tensor(faded1[:, half], old_sb[1][:, half], fade_sb[:, half], ALU.mult)
+
+        faded_t = keep.tile([P, CHUNKS, 2, P], F32, name="faded_t")
+        turn_tags = ["m", "f0", "s0", "s1"]
+        for k in range(CHUNKS // 2):
+            bank = psum.tile([P, 2, 2, P], F32, name="old_t%d" % k, tag=turn_tags[k])
+            for u in range(2):
+                c = 2 * k + u
+                for j in range(2):
+                    nc.tensor.transpose(bank[:, u, j, :], old_late[:, j, c * P : (c + 1) * P], ident[:])
+            for u in range(2):
+                c = 2 * k + u
+                nc.scalar.activation(faded_t[:, c, :, :], bank[:, u, :, :], ACT.Copy, scale=cols[:, c : c + 1])
+        back_tags = {2: ["f1", "m"], 3: ["ta", "tb"]}
+        faded = {}
+        for j in range(2, 4):
             for h in range(2):
                 bank = psum.tile([P, BANK], F32, name="faded%d_%d" % (j, h), tag=back_tags[j][h])
                 for c in range(4):
-                    nc.tensor.transpose(bank[:, c * P : (c + 1) * P], faded_t[:, 4 * h + c, j - 1, :], ident[:])
+                    nc.tensor.transpose(bank[:, c * P : (c + 1) * P], faded_t[:, 4 * h + c, j - 2, :], ident[:])
                 faded[j, h] = bank
-        result = [keep.tile([P, T], F32, name="result%d" % j) for j in range(1, 4)]
-        for h in range(2):
-            nc.scalar.copy(result[0][:, h * BANK : (h + 1) * BANK], faded[1, h][:])
+        result = [keep.tile([P, T], F32, name="result%d" % j) for j in range(2, 4)]
 
-        for j in range(4):
+        def scatter(j):
             window = windows[j % 3]
-            nc.vector.tensor_copy(window[:].indirect(offsets[:]), gv_sb[j][:])
-            for h in range(2):
-                half = slice(h * BANK, (h + 1) * BANK)
+            if j == 0:
+                for h in range(2):
+                    nc.vector.tensor_copy(window[:].indirect(offsets[:, 8 * h : 8 * h + 8]), gv_sb[j][:, h * P : (h + 1) * P])
+            else:
+                nc.vector.tensor_copy(window[:].indirect(offsets[:]), gv_sb[j][:])
+
+        def add_and_store(j):
+            window = windows[j % 3]
+            pieces = [(0, 512), (512, 768), (768, 1024)] if j == 3 else [(0, 512), (512, 1024)]
+            for lo, hi in pieces:
+                piece = slice(lo, hi)
                 if j < 2:
-                    dst = old_sb[0] if j == 0 else result[0]
-                    nc.gpsimd.tensor_tensor(dst[:, half], dst[:, half], window[:, half], ALU.add)
+                    dst = old_sb[0] if j == 0 else faded1
+                    nc.gpsimd.tensor_tensor(dst[:, piece], dst[:, piece], window[:, piece], ALU.add)
                 else:
-                    dst = result[j - 1]
-                    nc.vector.tensor_tensor(dst[:, half], faded[j, h][:], window[:, half], ALU.add)
-                nc.sync.dma_start(out[j * P : (j + 1) * P, half], dst[:, half])
+                    dst = result[j - 2]
+                    h = lo // BANK
+                    nc.vector.tensor_tensor(dst[:, piece], faded[j, h][:, lo - h * BANK : hi - h * BANK], window[:, piece], ALU.add)
+                nc.sync.dma_start(out[j * P : (j + 1) * P, piece], dst[:, piece])
+
+        scatter(0)
+        add_and_store(0)
+        scatter(1)
+        add_and_store(1)
+        scatter(2)
+        scatter(3)
+        add_and_store(2)
+        add_and_store(3)

from contextlib import ExitStack

import concourse.mybir as mybir

D, E, T, I, Q = 512, 512, 1024, 256, 512
FLOPS = 2 * D * Q * I + 2 * Q * E * I

F32 = mybir.dt.float32
BF16 = mybir.dt.bfloat16
I32 = mybir.dt.int32
U32 = mybir.dt.uint32
U16 = mybir.dt.uint16
U8 = mybir.dt.uint8
FP8X4 = mybir.dt.float8_e4m3fn_x4
FP4X4 = mybir.dt.float4_e2m1fn_x4
ALU = mybir.AluOpType
ACT = mybir.ActivationFunctionType

P = 128
PACK = 4
BANK = 512
CHUNKS = T // P
TINY = 2.0**-60


def tile_attend_bsoftthreshold_v_kernel(tc, query, keys_words, keys_scales, th, reserve, size, qs, grows, old, fade, offs, out):
    nc = tc.nc
    with ExitStack() as ctx:
        keep = ctx.enter_context(tc.tile_pool(name="keep", bufs=1))
        psum = ctx.enter_context(tc.psum_pool(name="psum", bufs=1))

        offsets = keep.tile([P, I // 16], U16, name="offsets")
        key_words = keep.tile([P, T], U16, name="key_words", tag="early_a")
        key_scales = keep.tile([P, T], U8, name="key_scales", tag="early_s")
        rows = keep.tile([P, P], F32, name="rows", tag="early_g")
        ident = keep.tile([P, P], F32, name="ident")
        q_raw = [keep.tile([P, PACK, Q // 2], F32, name="q_raw%d" % h, tag="early_q%d" % h) for h in range(2)]
        th_sb = keep.tile([P, PACK], F32, name="th_sb")

        nc.vector.memset(key_scales[:].bitcast(I32), 0)
        warm_in = keep.tile([P, 1], F32, name="warm_in")
        nc.vector.memset(warm_in[:], 0.0)
        ones = keep.tile([P, P], F32, name="ones")
        count = keep.tile([P, P], F32, name="count", align_bytes=64, tag="count_window")
        count_t = keep.tile([P, 32], F32, name="count_t", align_bytes=64)
        nc.vector.memset(ones[:], 1.0)
        nc.vector.tensor_tensor_scan(count[:], ones[:], ones[:], 0.0, ALU.mult, ALU.add)
        nc.vector.transpose(count_t[:], count[:, 0:32])
        for quad in range(4):
            part = slice(32 * quad, 32 * quad + 32)
            nc.vector.tensor_scalar(ident[part, :], count[part, :], -32.0 * quad, count_t[part, 0:1], ALU.add, ALU.is_equal)
        windows = [keep.tile([P, T], F32, name="window0", align_bytes=64, tag="count_window")]
        nc.vector.memset(windows[0][:], 0.0)

        q_view = query.rearrange("(p j) q -> p j q", j=PACK)
        g_view = grows.rearrange("(p j) e -> p j e", j=PACK)
        nc.sync.dma_start(offsets[:], offs)
        nc.sync.dma_start(key_words[:].bitcast(I32), keys_words[0].bitcast(I32))
        nc.sync.dma_start(q_raw[0][:], q_view[:, :, 0 : Q // 2])
        nc.sync.dma_start(q_raw[1][:], q_view[:, :, Q // 2 : Q])
        nc.scalar.dma_start(rows[0:CHUNKS, :], fade.rearrange("o (c p) -> (o c) p", p=P))
        nc.scalar.dma_start(rows[CHUNKS : CHUNKS + 2, :], size.rearrange("o (c p) -> (o c) p", p=P))
        for quad in range(4):
            nc.scalar.dma_start(
                key_scales[32 * quad : 32 * quad + 4, :].bitcast(I32),
                keys_scales[0, 4 * quad : 4 * quad + 4, :].bitcast(I32),
            )
        nc.scalar.dma_start(th_sb[:], th.rearrange("(s r) o -> s (r o)", r=PACK))
        warm = keep.tile([P, 1], F32, name="warm")
        nc.scalar.activation(warm[:], warm_in[:], ACT.Sigmoid)


        key_words_g = keep.tile([P, I], U16, name="key_words_g", align_bytes=64)
        key_scales_g = keep.tile([P, I], U8, name="key_scales_g", align_bytes=64)
        nc.vector.tensor_copy(key_words_g[:], key_words[:].indirect(offsets[:]))

        turned = psum.tile([P, P], F32, name="turned", tag="m")
        nc.tensor.transpose(turned[:], rows[:], ident[:])
        g_raw = [keep.tile([P, PACK, E // 2], F32, name="g_raw%d" % h, tag=["early_g", "early_a"][h]) for h in range(2)]
        for h in range(2):
            nc.sync.dma_start(g_raw[h][:], g_view[:, :, h * (E // 2) : (h + 1) * (E // 2)])
        cols = keep.tile([P, CHUNKS + 2], F32, name="cols")
        nc.vector.tensor_copy(cols[:], turned[:, 0 : CHUNKS + 2])
        size_b = psum.tile([P, I], F32, name="size_b", tag="n")
        for c in range(2):
            nc.tensor.transpose(size_b[:, c * P : (c + 1) * P], cols[:, CHUNKS + c : CHUNKS + c + 1].to_broadcast([P, P]), ident[:])
        fade_b = [psum.tile([P, BANK], F32, name="fade_b%d" % h, tag="f%d" % h) for h in range(2)]
        for c in range(CHUNKS):
            nc.tensor.transpose(fade_b[c // 4][:, (c % 4) * P : (c % 4 + 1) * P], cols[:, c : c + 1].to_broadcast([P, P]), ident[:])

        q_grouped = keep.tile([P, PACK, P, PACK], BF16, name="q_grouped", align_bytes=64)
        q_codes = keep.tile([P, Q], U32, name="q_codes", align_bytes=64, tag="codes_logs")
        q_scales = keep.tile([P, Q], U8, name="q_scales", align_bytes=64)

        def deal_query(h, pair):
            dst = q_grouped[:, 2 * pair : 2 * pair + 2, 64 * h : 64 * h + 64, :].rearrange("p r s j -> p s j r")
            src = q_raw[h][:].rearrange("p j (s r) -> p s j r", r=PACK)[:, :, :, 2 * pair : 2 * pair + 2]
            if pair == 0 or h == 0:
                nc.vector.tensor_scalar(dst, src, -1.0, None, ALU.mult)
            else:
                nc.scalar.activation(dst, src, ACT.Copy, scale=-1.0)

        deal_query(0, 0)
        deal_query(0, 1)
        nc.vector.tensor_copy(key_scales_g[:], key_scales[:].indirect(offsets[:]))
        deal_query(1, 0)
        deal_query(1, 1)
        old_sb = [keep.tile([P, T], F32, name="old%d" % j, tag="early_q%d" % j) for j in range(2)]
        for j in range(2):
            nc.sync.dma_start(old_sb[j][:], old[j * P : (j + 1) * P, :])
        vectors = keep.tile([P, 2, 8], F32, name="vectors", tag="early_s")
        res_sb = vectors[:, 0, 0:PACK]
        qs_sb = vectors[:, 1, 0:PACK]
        nc.sync.dma_start(res_sb, reserve.rearrange("(s r) o -> s (r o)", r=PACK))
        nc.sync.dma_start(qs_sb, qs.rearrange("(s r) o -> s (r o)", r=PACK))
        for pair in range(2):
            nc.vector.quantize_mx(
                out=q_codes[:, 256 * pair : 256 * (pair + 1)].bitcast(FP8X4),
                scales=q_scales[:, 256 * pair : 256 * (pair + 1)],
                in_=q_grouped[:, 2 * pair : 2 * pair + 2, :, :].rearrange("p r s j -> p (r s j)"),
            )

        score_tags = ["s0", "s1", "ta", "tb"]
        scores = [psum.tile([P, I], F32, name="scores%d" % r, tag=score_tags[r]) for r in range(PACK)]
        sig = keep.tile([P, PACK, I], F32, name="sig", tag="sig_fade")
        for r in range(PACK):
            nc.tensor.matmul_mx(
                out=scores[r][:],
                lhsT=q_codes[:, r * P : (r + 1) * P].bitcast(FP8X4),
                lhsT_scale=q_scales[:, r * P : (r + 1) * P],
                rhs=key_words_g[:].bitcast(FP4X4),
                rhs_scale=key_scales_g[:],
                start=True,
                stop=True,
            )
            nc.scalar.activation(sig[:, r, :], scores[r][:], ACT.Sigmoid, bias=th_sb[:, r : r + 1])

        g_grouped = keep.tile([P, E, PACK], BF16, name="g_grouped", align_bytes=64, tag="grouped_window")
        g_codes = keep.tile([P, E], U32, name="g_codes", align_bytes=64)
        g_scales = keep.tile([P, E], U8, name="g_scales", align_bytes=64)
        for h in range(2):
            nc.vector.tensor_copy(
                g_grouped[:, 256 * h : 256 * (h + 1), :].rearrange("p (c i) j -> p c j i", i=4),
                g_raw[h][:].rearrange("p j (c i) -> p c j i", i=4),
            )
        old_late = keep.tile([P, 2, T], F32, name="old_late", tag="early_g")
        nc.sync.dma_start(old_late[:], old[2 * P : 4 * P, :].rearrange("(j p) t -> p j t", p=P))
        nc.vector.quantize_mx(out=g_codes[:].bitcast(FP8X4), scales=g_scales[:], in_=g_grouped[:].rearrange("p e j -> p (e j)"))
        windows.append(keep.tile([P, T], F32, name="window1", align_bytes=64, tag="grouped_window"))
        nc.gpsimd.memset(windows[1][:], 0.0)
        for h in range(2):
            half = slice(h * BANK, (h + 1) * BANK)
            nc.vector.tensor_tensor(old_sb[0][:, half], old_sb[0][:, half], fade_b[h][:], ALU.mult)

        logs = keep.tile([P, PACK, I], F32, name="logs", align_bytes=64, tag="codes_logs")
        neg_p = keep.tile([P, PACK, I], F32, name="neg_p")
        neg_sum = keep.tile([P, PACK], F32, name="neg_sum")
        neg_z = keep.tile([P, PACK], F32, name="neg_z")
        neg_rz = keep.tile([P, PACK], F32, name="neg_rz")
        neg_c = keep.tile([P, PACK], F32, name="neg_c")
        w_planes = keep.tile([P, PACK, I], BF16, name="w_planes")
        for r in range(PACK):
            nc.scalar.activation(logs[:, r, :], sig[:, r, :], ACT.Ln, bias=TINY)
        fade_sb = keep.tile([P, T], F32, name="fade_sb", tag="sig_fade")
        for h in range(2):
            nc.scalar.copy(fade_sb[:, h * BANK : (h + 1) * BANK], fade_b[h][:])

        def parts(r):
            nc.vector.scalar_tensor_tensor(
                neg_p[:, r, :], scores[r][:], th_sb[:, r : r + 1], logs[:, r, :], ALU.add, ALU.min, accum_out=neg_sum[:, r : r + 1]
            )

        def add_reserve(pair):
            two = slice(2 * pair, 2 * pair + 2)
            nc.vector.tensor_tensor(neg_z[:, two], neg_sum[:, two], res_sb[:, two], ALU.subtract)

        def invert(pair):
            two = slice(2 * pair, 2 * pair + 2)
            nc.vector.reciprocal(neg_rz[:, two], neg_z[:, two])

        def row_scale(pair):
            two = slice(2 * pair, 2 * pair + 2)
            nc.vector.tensor_tensor(neg_c[:, two], neg_rz[:, two], qs_sb[:, two], ALU.mult)

        def weights(r, h):
            slots = slice(h * P, (h + 1) * P)
            nc.vector.scalar_tensor_tensor(w_planes[:, r, slots], neg_p[:, r, slots], neg_c[:, r : r + 1], size_b[:, slots], ALU.mult, ALU.mult)

        w_grouped = keep.tile([P, I, PACK], BF16, name="w_grouped", align_bytes=64, tag="w_then_x1")
        w_codes = keep.tile([P, I], U32, name="w_codes", align_bytes=64)
        w_scales = keep.tile([P, I], U8, name="w_scales", align_bytes=64)

        def interleave(h):
            slots = slice(h * P, (h + 1) * P)
            nc.vector.tensor_copy(
                w_grouped[:, slots, :].rearrange("p (c i) r -> p c r i", i=4),
                w_planes[:, :, slots].rearrange("p r (c i) -> p c r i", i=4),
            )

        def quantise(h):
            slots = slice(h * P, (h + 1) * P)
            nc.vector.quantize_mx(
                out=w_codes[:, slots].bitcast(FP8X4), scales=w_scales[:, slots], in_=w_grouped[:, slots, :].rearrange("p i r -> p (i r)")
            )

        parts(0)
        parts(1)
        add_reserve(0)
        parts(2)
        invert(0)
        parts(3)
        windows.append(keep.tile([P, T], F32, name="window2", align_bytes=64, tag="codes_logs"))
        nc.gpsimd.memset(windows[2][:], 0.0)
        row_scale(0)
        add_reserve(1)
        weights(0, 0)
        invert(1)
        weights(1, 0)
        row_scale(1)
        weights(0, 1)
        weights(2, 0)
        weights(3, 0)
        weights(1, 1)
        interleave(0)
        weights(2, 1)
        weights(3, 1)
        quantise(0)
        interleave(1)
        quantise(1)

        gv_sb = [keep.tile([P, I], F32, name="gv%d" % j) for j in range(4)]
        gv_tags = ["s0", "s1", "ta", "tb"]

        def gradient(j, slots, tag):
            gv = psum.tile([P, slots.stop - slots.start], F32, name="gv_ps%d_%d" % (j, slots.start), tag=tag)
            nc.tensor.matmul_mx(
                out=gv[:],
                lhsT=g_codes[:, j * P : (j + 1) * P].bitcast(FP8X4),
                lhsT_scale=g_scales[:, j * P : (j + 1) * P],
                rhs=w_codes[:, slots].bitcast(FP8X4),
                rhs_scale=w_scales[:, slots],
                start=True,
                stop=True,
            )
            nc.scalar.copy(gv_sb[j][:, slots], gv[:])

        gradient(0, slice(0, P), "s0")
        gradient(0, slice(P, I), "n")
        for j in range(1, 4):
            gradient(j, slice(0, I), gv_tags[j])

        faded1 = keep.tile([P, T], F32, name="faded1", align_bytes=64, tag="w_then_x1")
        for h in range(2):
            half = slice(h * BANK, (h + 1) * BANK)
            nc.gpsimd.tensor_tensor(faded1[:, half], old_sb[1][:, half], fade_sb[:, half], ALU.mult)

        faded_t = keep.tile([P, CHUNKS, 2, P], F32, name="faded_t")
        turn_tags = ["m", "f0", "s0", "s1"]
        for k in range(CHUNKS // 2):
            bank = psum.tile([P, 2, 2, P], F32, name="old_t%d" % k, tag=turn_tags[k])
            for u in range(2):
                c = 2 * k + u
                for j in range(2):
                    nc.tensor.transpose(bank[:, u, j, :], old_late[:, j, c * P : (c + 1) * P], ident[:])
            for u in range(2):
                c = 2 * k + u
                nc.scalar.activation(faded_t[:, c, :, :], bank[:, u, :, :], ACT.Copy, scale=cols[:, c : c + 1])
        back_tags = {2: ["f1", "m"], 3: ["ta", "tb"]}
        faded = {}
        for j in range(2, 4):
            for h in range(2):
                bank = psum.tile([P, BANK], F32, name="faded%d_%d" % (j, h), tag=back_tags[j][h])
                for c in range(4):
                    nc.tensor.transpose(bank[:, c * P : (c + 1) * P], faded_t[:, 4 * h + c, j - 2, :], ident[:])
                faded[j, h] = bank
        result = [keep.tile([P, T], F32, name="result%d" % j) for j in range(2, 4)]

        def scatter(j):
            window = windows[j % 3]
            if j == 0:
                for h in range(2):
                    nc.vector.tensor_copy(window[:].indirect(offsets[:, 8 * h : 8 * h + 8]), gv_sb[j][:, h * P : (h + 1) * P])
            else:
                nc.vector.tensor_copy(window[:].indirect(offsets[:]), gv_sb[j][:])

        def add_and_store(j):
            window = windows[j % 3]
            pieces = [(0, 512), (512, 768), (768, 1024)] if j == 3 else [(0, 512), (512, 1024)]
            for lo, hi in pieces:
                piece = slice(lo, hi)
                if j < 2:
                    dst = old_sb[0] if j == 0 else faded1
                    nc.gpsimd.tensor_tensor(dst[:, piece], dst[:, piece], window[:, piece], ALU.add)
                else:
                    dst = result[j - 2]
                    h = lo // BANK
                    nc.vector.tensor_tensor(dst[:, piece], faded[j, h][:, lo - h * BANK : hi - h * BANK], window[:, piece], ALU.add)
                nc.sync.dma_start(out[j * P : (j + 1) * P, piece], dst[:, piece])

        scatter(0)
        add_and_store(0)
        scatter(1)
        add_and_store(1)
        scatter(2)
        scatter(3)
        add_and_store(2)
        add_and_store(3)
